import numpy as np
import ml_dtypes


def mxq(x, axis, fmt="e4m3"):
    dtype, down = {"e4m3": (ml_dtypes.float8_e4m3fn, 7), "e5m2": (ml_dtypes.float8_e5m2, 14)}[fmt]
    v = np.moveaxis(np.asarray(x, np.float32).astype(ml_dtypes.bfloat16).astype(np.float64), axis, -1)
    blocks = v.reshape(v.shape[:-1] + (-1, 32))
    amax = np.abs(blocks).max(-1, keepdims=True)
    byte = np.maximum(np.where(amax > 0, np.frexp(amax)[1] - 1 + 127, 0) - down, 1)
    scale = np.exp2(byte - 127.0)
    codes = (blocks / scale).astype(np.float32).astype(dtype).astype(np.float64)
    return np.moveaxis((codes * scale).reshape(v.shape), -1, axis)


WIDE = False


def mx_kscale(k):
    if not WIDE:
        return np.ones(k)
    levels = np.array([10, -10, 5, -5, 0])
    if k % 512:
        return np.exp2(np.random.permutation(np.resize(levels, k // 32))).repeat(32)
    a = np.empty((k // 512, 16))
    for p in range(k // 512):
        a[p, :8] = np.random.permutation(np.resize(levels, 8))
        for g in range(8):
            far = levels[np.abs(levels - a[p, g]) >= 10]
            a[p, g + 8] = far[np.random.randint(len(far))]
    return np.exp2(a.ravel()).repeat(32)


def f64(x):
    return np.asarray(x).astype(np.float64)


def striped(idx):
    return np.tile(np.asarray(idx).reshape(-1, 16).T, (8, 1)).astype(np.uint16)


def unstriped(offs):
    return offs[:16].T.reshape(-1).astype(np.int64)


E2M1 = np.array([0.0, 0.5, 1.0, 1.5, 2.0, 3.0, 4.0, 6.0, -0.0, -0.5, -1.0, -1.5, -2.0, -3.0, -4.0, -6.0])


def pack_weight(w, fmt):
    k, n = w.shape
    w = f64(np.asarray(w, np.float32).astype(ml_dtypes.bfloat16)).reshape(k // 32, 32, n)
    amax = np.abs(w).max(1)
    if fmt == "e4m3":
        byte = np.frexp(amax)[1] - 1 + 127 - 7
    else:
        mant, ex = np.frexp(amax / 6.0)
        byte = np.where(mant > 0.5, ex, ex - 1) + 127
    byte = np.clip(np.where(amax > 0, byte, 1), 1, 254)
    scaled = (w * np.exp2(127.0 - byte)[:, None, :]).reshape(k, n).astype(np.float32)
    by_word = np.ascontiguousarray(scaled.reshape(k // 512, 128, 4, n).transpose(0, 1, 3, 2))
    if fmt == "e4m3":
        words = by_word.astype(ml_dtypes.float8_e4m3fn).view(np.uint8)
    else:
        c = by_word.astype(ml_dtypes.float4_e2m1fn).view(np.uint8) & 0xF
        words = (c[..., 0::2] | (c[..., 1::2] << 4)).reshape(k // 512, 128, 2 * n)
    return np.ascontiguousarray(words), np.ascontiguousarray(byte.astype(np.uint8).reshape(k // 512, 16, n))


def unpack_weight(words, scales, fmt):
    g, _, n = scales.shape
    words = np.ascontiguousarray(words).reshape(g, 128, n, -1)
    if fmt == "e4m3":
        vals = words.view(ml_dtypes.float8_e4m3fn).astype(np.float64)
    else:
        nib = np.empty((g, 128, n, 4), np.uint8)
        nib[..., 0::2] = words & 0xF
        nib[..., 1::2] = words >> 4
        vals = E2M1[nib]
    vals = vals * np.repeat(np.exp2(scales.astype(np.float64) - 127.0), 8, axis=1)[..., None]
    return vals.transpose(0, 1, 3, 2).reshape(g * 512, n)


def sigmoid(v):
    return 1.0 / (1.0 + np.exp(-v))


K, T, J, N = 1024, 1024, 512, 512


def setup_inputs():
    n = np.random.standard_normal
    idx = np.random.permutation(T)[:J]
    fk = mx_kscale(K)
    xtp = pack_weight(n((K, T)) / fk[:, None], "e4m3")
    wgp = pack_weight(n((K, N)) * 1 / np.sqrt(K) * fk[:, None], "e2m1")
    return {
        "xt_words": xtp[0],
        "xt_scales": xtp[1],
        "wa": (n((K, N)) * 1 / np.sqrt(K) * fk[:, None]).astype(np.float32),
        "wg_words": wgp[0],
        "wg_scales": wgp[1],
        "old": (1.0 * n((N, T))).astype(np.float32),
        "offs": striped(idx),
    }


def reference(xt_words, xt_scales, wa, wg_words, wg_scales, old, offs):
    idx = unstriped(offs)
    xtu = unpack_weight(xt_words, xt_scales, "e4m3")
    wgu = unpack_weight(wg_words, wg_scales, "e2m1")
    waq = mxq(f64(wa), 0, "e4m3")
    xtidxg = xtu[:, idx]
    a = waq.T @ xtidxg
    g = wgu.T @ xtidxg
    d = f64(old)[:, idx] * sigmoid(g) - f64(old)[:, idx] + a
    dp = np.zeros((N, T))
    dp[:, idx] = d
    y = f64(old) + dp
    return y

@@ -1,0 +1,177 @@
+from contextlib import ExitStack
+
+import concourse.mybir as mybir
+
+K, T, J, N = 1024, 1024, 512, 512
+FLOPS = 2 * 2 * K * N * J
+
+F32 = mybir.dt.float32
+BF16 = mybir.dt.bfloat16
+I32 = mybir.dt.int32
+U32 = mybir.dt.uint32
+U16 = mybir.dt.uint16
+U8 = mybir.dt.uint8
+FP8X4 = mybir.dt.float8_e4m3fn_x4
+FP4X4 = mybir.dt.float4_e2m1fn_x4
+ACT = mybir.ActivationFunctionType
+ALU = mybir.AluOpType
+
+P = 128
+PACK = 4
+PASSES = K // (P * PACK)
+BLOCKS = N // P
+BANK = 512
+
+
+def tile_moe_expert_page_fades_where_written_kernel(tc, xt_words, xt_scales, wa, wg_words, wg_scales, old, offs, out):
+    nc = tc.nc
+    with ExitStack() as ctx:
+        lists = ctx.enter_context(tc.tile_pool(name="lists", bufs=1))
+        keep = ctx.enter_context(tc.tile_pool(name="keep", bufs=1))
+        sums = ctx.enter_context(tc.psum_pool(name="sums", bufs=1))
+
+        def sbuf(shape, dtype, name, tag=None):
+            if tag is not None and not isinstance(tag, str):
+                return tag
+            return keep.tile(shape, dtype, name=name, tag=tag or name, align_bytes=64)
+
+        offsets = lists.tile([P, J // 16], U16, name="offsets")
+        nc.sync.dma_start(offsets[:], offs)
+
+        x_plane = sbuf([P, PASSES * T], U8, "x_plane")
+        g_plane = sbuf([P, PASSES * N], U8, "g_plane")
+        nc.gpsimd.memset(x_plane[:].bitcast(I32), 0)
+        nc.vector.memset(g_plane[:].bitcast(I32), 0)
+        pages = [sbuf([P, T], F32, "page%d" % i) for i in range(1)]
+        for page in pages:
+            nc.vector.memset(page[:], 0.0)
+        warm = sbuf([P, 1], F32, "warm")
+        nc.scalar.activation(warm[:], pages[0][:, 0:1], ACT.Sigmoid)
+
+        def load_scale_rows(plane, scales):
+            rows = scales.bitcast(I32)
+            for q in range(4):
+                nc.sync.dma_start(
+                    plane[32 * q : 32 * q + 4, :].bitcast(I32).rearrange("r (a n) -> r a n", a=PASSES),
+                    rows[:, 4 * q : 4 * q + 4, :].rearrange("a r n -> r a n"),
+                )
+
+        g_words = sbuf([P, PASSES, 2 * N], U8, "g_words")
+        nc.sync.dma_start(g_words[:].bitcast(I32), wg_words.bitcast(I32).rearrange("a p n -> p a n"))
+        load_scale_rows(x_plane, xt_scales)
+        x_words = sbuf([P, PASSES, T], U32, "x_words")
+        nc.sync.dma_start(x_words[:].bitcast(I32), xt_words.rearrange("a p n t -> p a (n t)").bitcast(I32))
+
+        old_sb = [sbuf([P, T], F32, "old%d" % b) for b in range(BLOCKS)]
+        w_raw = [[sbuf([P, PACK, P], F32, "raw%d_%d" % (b, a)) for a in range(PASSES)] for b in range(BLOCKS)]
+
+        def load_old(b):
+            nc.sync.dma_start(old_sb[b][:], old[b * P : (b + 1) * P, :])
+
+        def load_wa(b):
+            for a in range(PASSES):
+                rows = wa[a * P * PACK : (a + 1) * P * PACK, b * P : (b + 1) * P]
+                nc.sync.dma_start(w_raw[b][a][:], rows.rearrange("(p j) n -> p j n", j=PACK))
+
+        load_wa(0)
+        load_old(0)
+        load_scale_rows(g_plane, wg_scales)
+        for b in range(1, BLOCKS):
+            load_wa(b)
+            load_old(b)
+
+        xg_words = [sbuf([P, J], U32, "xg_words%d" % a) for a in range(PASSES)]
+        xg_plane = [sbuf([P, J], U8, "xg_plane%d" % a) for a in range(PASSES)]
+        for a in range(PASSES):
+            nc.vector.tensor_copy(xg_plane[a][:], x_plane[:, a * T : (a + 1) * T].indirect(offsets[:]))
+        a_planes = [t[:] for t in xg_plane]
+        g_planes = a_planes
+        for a in range(PASSES):
+            nc.vector.tensor_copy(xg_words[a][:], x_words[:, a, :].indirect(offsets[:]))
+
+        w_bf, w_codes, w_plane, lost, fade, faded, answer, turned, turned_sb = {}, {}, {}, {}, {}, {}, {}, {}, {}
+
+        def cast(b, tag=None):
+            w_bf[b] = sbuf([P, PASSES, P * PACK], BF16, "bf%d" % b, tag)
+            for a in range(PASSES):
+                nc.scalar.copy(
+                    w_bf[b][:, a, :].rearrange("p (c i t) -> p c t i", i=4, t=PACK),
+                    w_raw[b][a][:].rearrange("p t (c i) -> p c t i", i=4),
+                )
+
+        def quantise(b, tag=None):
+            w_codes[b] = sbuf([P, PASSES * P], U32, "codes%d" % b, tag)
+            w_plane[b] = sbuf([P, PASSES * P], U8, "w_plane%d" % b)
+            nc.vector.quantize_mx(
+                out=w_codes[b][:].bitcast(FP8X4), scales=w_plane[b][:], in_=w_bf[b][:].rearrange("p a c -> p (a c)")
+            )
+
+        def gate(b, bank, tag=None, negate=True):
+            acc = sums.tile([P, J], F32, name="g_acc", tag=bank)
+            for a in range(PASSES):
+                nc.tensor.matmul_mx(
+                    out=acc[:],
+                    lhsT=g_words[:, a, 2 * b * P : 2 * (b + 1) * P].bitcast(FP4X4),
+                    lhsT_scale=g_plane[:, a * N + b * P : a * N + (b + 1) * P],
+                    rhs=xg_words[a][:].bitcast(FP8X4),
+                    rhs_scale=g_planes[a],
+                    start=(a == 0),
+                    stop=(a == PASSES - 1),
+                )
+            lost[b] = sbuf([P, J], F32, "lost%d" % b, tag)
+            nc.scalar.activation(lost[b][:], acc[:], ACT.Sigmoid, scale=-1.0)
+            if negate:
+                fade[b] = sbuf([P, J], F32, "fade%d" % b)
+                nc.scalar.activation(fade[b][:], lost[b][:], ACT.Copy, scale=-1.0)
+
+        def expert(b, bank, tag=None, sign=1.0):
+            acc = sums.tile([P, J], F32, name="a_acc", tag=bank)
+            for a in range(PASSES):
+                nc.tensor.matmul_mx(
+                    out=acc[:],
+                    lhsT=w_codes[b][:, a * P : (a + 1) * P].bitcast(FP8X4),
+                    lhsT_scale=w_plane[b][:, a * P : (a + 1) * P],
+                    rhs=xg_words[a][:].bitcast(FP8X4),
+                    rhs_scale=a_planes[a],
+                    start=(a == 0),
+                    stop=(a == PASSES - 1),
+                )
+            answer[b] = sbuf([P, J], F32, "answer%d" % b, tag)
+            nc.scalar.activation(answer[b][:], acc[:], ACT.Copy, scale=sign)
+
+        def fade_first(b):
+            picked = sbuf([P, J], F32, "picked")
+            faded[b] = sbuf([P, J], F32, "faded%d" % b)
+            nc.vector.tensor_copy(picked[:], old_sb[b][:].indirect(offsets[:]))
+            nc.vector.scalar_tensor_tensor(faded[b][:], lost[b][:], 1.0, picked[:], ALU.mult, ALU.mult)
+
+        def fade_old(b, tag=None, factor=None):
+            faded[b] = sbuf([P, J], F32, "faded%d" % b, tag)
+            nc.vector.tensor_tensor(faded[b][:], old_sb[b][:].indirect(offsets[:]), (factor or fade)[b][:], ALU.mult)
+
+        def scatter(b):
+            nc.vector.tensor_tensor(pages[0][:].indirect(offsets[:]), faded[b][:], answer[b][:], ALU.add)
+
+        def add_on_vector(b, op, pieces):
+            width = T // pieces
+            for h in range(pieces):
+                cols = slice(h * width, (h + 1) * width)
+                result = sbuf([P, width], F32, "result%d_%d" % (b, h))
+                nc.vector.tensor_tensor(result[:], old_sb[b][:, cols], pages[0][:, cols], op)
+                nc.sync.dma_start(out[b * P : (b + 1) * P, cols], result[:])
+
+        cast(0)
+        quantise(0)
+        gate(0, "y", "raw0_1", negate=False)
+        expert(0, "w", sign=-1.0)
+        fade_first(0)
+        scatter(0)
+        for b in range(1, BLOCKS):
+            cast(b)
+            gate(b, "g%d" % b, "raw%d_1" % b, negate=False)
+            quantise(b, "faded0" if b == 1 else "answer%d" % (b - 2))
+            expert(b, "a%d" % b, sign=-1.0)
+            add_on_vector(b - 1, ALU.subtract, 1)
+            fade_old(b, "answer%d" % (b - 1), factor=lost)
+            scatter(b)
+        add_on_vector(3, ALU.subtract, 2)

@@ -20,7 +20,7 @@ P = 128
 PACK = 4
 PASSES = K // (P * PACK)
 BLOCKS = N // P
-BANK = 512
+LAST_PIECES = 2
 
 
 def tile_moe_expert_page_fades_where_written_kernel(tc, xt_words, xt_scales, wa, wg_words, wg_scales, old, offs, out):
@@ -30,19 +30,17 @@ def tile_moe_expert_page_fades_where_written_kernel(tc, xt_words, xt_scales, wa,
         keep = ctx.enter_context(tc.tile_pool(name="keep", bufs=1))
         sums = ctx.enter_context(tc.psum_pool(name="sums", bufs=1))
 
-        def sbuf(shape, dtype, name, tag=None):
-            if tag is not None and not isinstance(tag, str):
-                return tag
-            return keep.tile(shape, dtype, name=name, tag=tag or name, align_bytes=64)
+        def sbuf(shape, dtype, name, place=None):
+            return keep.tile(shape, dtype, name=name, tag=place or name, align_bytes=64)
 
         offsets = lists.tile([P, J // 16], U16, name="offsets")
         nc.sync.dma_start(offsets[:], offs)
 
         x_plane = sbuf([P, PASSES * T], U8, "x_plane")
         g_plane = sbuf([P, PASSES * N], U8, "g_plane")
+        pages = [sbuf([P, T], F32, "page%d" % i) for i in range(2)]
         nc.gpsimd.memset(x_plane[:].bitcast(I32), 0)
         nc.vector.memset(g_plane[:].bitcast(I32), 0)
-        pages = [sbuf([P, T], F32, "page%d" % i) for i in range(1)]
         for page in pages:
             nc.vector.memset(page[:], 0.0)
         warm = sbuf([P, 1], F32, "warm")
@@ -56,122 +54,117 @@ def tile_moe_expert_page_fades_where_written_kernel(tc, xt_words, xt_scales, wa,
                     rows[:, 4 * q : 4 * q + 4, :].rearrange("a r n -> r a n"),
                 )
 
+        def load_wa(a, first, count, name, place=None):
+            raw = sbuf([P, PACK, count], F32, name, place)
+            rows = wa[a * P * PACK : (a + 1) * P * PACK, first : first + count]
+            nc.sync.dma_start(raw[:], rows.rearrange("(p j) n -> p j n", j=PACK))
+            return raw
+
+        def load_old(b, place=None):
+            rows = sbuf([P, T], F32, "old%d" % b, place)
+            nc.sync.dma_start(rows[:], old[b * P : (b + 1) * P, :])
+            return rows
+
         g_words = sbuf([P, PASSES, 2 * N], U8, "g_words")
         nc.sync.dma_start(g_words[:].bitcast(I32), wg_words.bitcast(I32).rearrange("a p n -> p a n"))
         load_scale_rows(x_plane, xt_scales)
         x_words = sbuf([P, PASSES, T], U32, "x_words")
         nc.sync.dma_start(x_words[:].bitcast(I32), xt_words.rearrange("a p n t -> p a (n t)").bitcast(I32))
-
-        old_sb = [sbuf([P, T], F32, "old%d" % b) for b in range(BLOCKS)]
-        w_raw = [[sbuf([P, PACK, P], F32, "raw%d_%d" % (b, a)) for a in range(PASSES)] for b in range(BLOCKS)]
-
-        def load_old(b):
-            nc.sync.dma_start(old_sb[b][:], old[b * P : (b + 1) * P, :])
-
-        def load_wa(b):
-            for a in range(PASSES):
-                rows = wa[a * P * PACK : (a + 1) * P * PACK, b * P : (b + 1) * P]
-                nc.sync.dma_start(w_raw[b][a][:], rows.rearrange("(p j) n -> p j n", j=PACK))
-
-        load_wa(0)
-        load_old(0)
+        first_raw = [load_wa(0, 0, P, "first_raw0")]
         load_scale_rows(g_plane, wg_scales)
-        for b in range(1, BLOCKS):
-            load_wa(b)
-            load_old(b)
+        first_raw.append(load_wa(1, 0, P, "first_raw1"))
+        old_sb = {0: load_old(0)}
 
-        xg_words = [sbuf([P, J], U32, "xg_words%d" % a) for a in range(PASSES)]
         xg_plane = [sbuf([P, J], U8, "xg_plane%d" % a) for a in range(PASSES)]
+        xg_words = [sbuf([P, J], U32, "xg_words%d" % a) for a in range(PASSES)]
         for a in range(PASSES):
             nc.vector.tensor_copy(xg_plane[a][:], x_plane[:, a * T : (a + 1) * T].indirect(offsets[:]))
-        a_planes = [t[:] for t in xg_plane]
-        g_planes = a_planes
         for a in range(PASSES):
             nc.vector.tensor_copy(xg_words[a][:], x_words[:, a, :].indirect(offsets[:]))
 
-        w_bf, w_codes, w_plane, lost, fade, faded, answer, turned, turned_sb = {}, {}, {}, {}, {}, {}, {}, {}, {}
-
-        def cast(b, tag=None):
-            w_bf[b] = sbuf([P, PASSES, P * PACK], BF16, "bf%d" % b, tag)
+        def cast(b, raw, place):
+            rounded = sbuf([P, PASSES, P * PACK], BF16, "rounded%d" % b, place)
             for a in range(PASSES):
                 nc.scalar.copy(
-                    w_bf[b][:, a, :].rearrange("p (c i t) -> p c t i", i=4, t=PACK),
-                    w_raw[b][a][:].rearrange("p t (c i) -> p c t i", i=4),
+                    rounded[:, a, :].rearrange("p (c i t) -> p c t i", i=4, t=PACK),
+                    raw[a].rearrange("p t (c i) -> p c t i", i=4),
                 )
+            return rounded
 
-        def quantise(b, tag=None):
-            w_codes[b] = sbuf([P, PASSES * P], U32, "codes%d" % b, tag)
-            w_plane[b] = sbuf([P, PASSES * P], U8, "w_plane%d" % b)
+        def quantise(b, rounded):
+            codes = sbuf([P, PASSES * P], U32, "codes%d" % b)
+            plane = sbuf([P, PASSES * P], U8, "w_plane%d" % b)
             nc.vector.quantize_mx(
-                out=w_codes[b][:].bitcast(FP8X4), scales=w_plane[b][:], in_=w_bf[b][:].rearrange("p a c -> p (a c)")
+                out=codes[:].bitcast(FP8X4), scales=plane[:], in_=rounded[:].rearrange("p a c -> p (a c)")
             )
+            return codes, plane
 
-        def gate(b, bank, tag=None, negate=True):
-            acc = sums.tile([P, J], F32, name="g_acc", tag=bank)
+        def product(bank, weights, scales):
+            acc = sums.tile([P, J], F32, name="acc", tag="bank%d" % bank)
             for a in range(PASSES):
                 nc.tensor.matmul_mx(
                     out=acc[:],
-                    lhsT=g_words[:, a, 2 * b * P : 2 * (b + 1) * P].bitcast(FP4X4),
-                    lhsT_scale=g_plane[:, a * N + b * P : a * N + (b + 1) * P],
+                    lhsT=weights[a],
+                    lhsT_scale=scales[a],
                     rhs=xg_words[a][:].bitcast(FP8X4),
-                    rhs_scale=g_planes[a],
+                    rhs_scale=xg_plane[a][:],
                     start=(a == 0),
                     stop=(a == PASSES - 1),
                 )
-            lost[b] = sbuf([P, J], F32, "lost%d" % b, tag)
-            nc.scalar.activation(lost[b][:], acc[:], ACT.Sigmoid, scale=-1.0)
-            if negate:
-                fade[b] = sbuf([P, J], F32, "fade%d" % b)
-                nc.scalar.activation(fade[b][:], lost[b][:], ACT.Copy, scale=-1.0)
+            return acc
 
-        def expert(b, bank, tag=None, sign=1.0):
-            acc = sums.tile([P, J], F32, name="a_acc", tag=bank)
-            for a in range(PASSES):
-                nc.tensor.matmul_mx(
-                    out=acc[:],
-                    lhsT=w_codes[b][:, a * P : (a + 1) * P].bitcast(FP8X4),
-                    lhsT_scale=w_plane[b][:, a * P : (a + 1) * P],
-                    rhs=xg_words[a][:].bitcast(FP8X4),
-                    rhs_scale=a_planes[a],
-                    start=(a == 0),
-                    stop=(a == PASSES - 1),
-                )
-            answer[b] = sbuf([P, J], F32, "answer%d" % b, tag)
-            nc.scalar.activation(answer[b][:], acc[:], ACT.Copy, scale=sign)
+        def gate(b, place=None):
+            acc = product(
+                b % 2,
+                [g_words[:, a, 2 * b * P : 2 * (b + 1) * P].bitcast(FP4X4) for a in range(PASSES)],
+                [g_plane[:, a * N + b * P : a * N + (b + 1) * P] for a in range(PASSES)],
+            )
+            lost = sbuf([P, J], F32, "lost%d" % b, place)
+            nc.scalar.activation(lost[:], acc[:], ACT.Sigmoid, scale=-1.0)
+            return lost
 
-        def fade_first(b):
-            picked = sbuf([P, J], F32, "picked")
-            faded[b] = sbuf([P, J], F32, "faded%d" % b)
-            nc.vector.tensor_copy(picked[:], old_sb[b][:].indirect(offsets[:]))
-            nc.vector.scalar_tensor_tensor(faded[b][:], lost[b][:], 1.0, picked[:], ALU.mult, ALU.mult)
+        def expert(b, codes, plane):
+            acc = product(
+                (b + 1) % 2,
+                [codes[:, a * P : (a + 1) * P].bitcast(FP8X4) for a in range(PASSES)],
+                [plane[:, a * P : (a + 1) * P] for a in range(PASSES)],
+            )
+            minus_a = sbuf([P, J], F32, "minus_a%d" % b)
+            nc.scalar.activation(minus_a[:], acc[:], ACT.Copy, scale=-1.0)
+            return minus_a
 
-        def fade_old(b, tag=None, factor=None):
-            faded[b] = sbuf([P, J], F32, "faded%d" % b, tag)
-            nc.vector.tensor_tensor(faded[b][:], old_sb[b][:].indirect(offsets[:]), (factor or fade)[b][:], ALU.mult)
+        def scatter(b, faded, minus_a):
+            nc.vector.tensor_tensor(pages[b % 2][:].indirect(offsets[:]), faded[:], minus_a[:], ALU.add)
 
-        def scatter(b):
-            nc.vector.tensor_tensor(pages[0][:].indirect(offsets[:]), faded[b][:], answer[b][:], ALU.add)
-
-        def add_on_vector(b, op, pieces):
+        def finish(b, pieces, place=None):
             width = T // pieces
-            for h in range(pieces):
-                cols = slice(h * width, (h + 1) * width)
-                result = sbuf([P, width], F32, "result%d_%d" % (b, h))
-                nc.vector.tensor_tensor(result[:], old_sb[b][:, cols], pages[0][:, cols], op)
+            for first in range(0, T, width):
+                cols = slice(first, first + width)
+                result = sbuf([P, width], F32, "result%d_%d" % (b, first), place)
+                nc.vector.tensor_tensor(result[:], old_sb[b][:, cols], pages[b % 2][:, cols], ALU.subtract)
                 nc.sync.dma_start(out[b * P : (b + 1) * P, cols], result[:])
 
-        cast(0)
-        quantise(0)
-        gate(0, "y", "raw0_1", negate=False)
-        expert(0, "w", sign=-1.0)
-        fade_first(0)
-        scatter(0)
+        rounded = cast(0, [raw[:] for raw in first_raw], "rounded0")
+        codes, plane = quantise(0, rounded)
+        lost = gate(0, "first_raw1")
+        minus_a = expert(0, codes, plane)
+        picked = sbuf([P, J], F32, "picked", "rounded0")
+        nc.vector.tensor_copy(picked[:], old_sb[0][:].indirect(offsets[:]))
+        faded = sbuf([P, J], F32, "faded0")
+        nc.vector.tensor_tensor(faded[:], lost[:], picked[:], ALU.mult)
+        scatter(0, faded, minus_a)
+
+        rest_raw = [load_wa(0, P, N - P, "rest_raw0", "first_raw0"), load_wa(1, P, N - P, "rest_raw1", "x_plane")]
+        for b, place in enumerate(["x_words", "rounded0", "first_raw1"], start=1):
+            old_sb[b] = load_old(b, place)
+
         for b in range(1, BLOCKS):
-            cast(b)
-            gate(b, "g%d" % b, "raw%d_1" % b, negate=False)
-            quantise(b, "faded0" if b == 1 else "answer%d" % (b - 2))
-            expert(b, "a%d" % b, sign=-1.0)
-            add_on_vector(b - 1, ALU.subtract, 1)
-            fade_old(b, "answer%d" % (b - 1), factor=lost)
-            scatter(b)
-        add_on_vector(3, ALU.subtract, 2)
+            rounded = cast(b, [raw[:, :, (b - 1) * P : b * P] for raw in rest_raw], "w_plane%d" % (b - 1))
+            lost = gate(b)
+            codes, plane = quantise(b, rounded)
+            minus_a = expert(b, codes, plane)
+            faded = sbuf([P, J], F32, "faded%d" % b)
+            nc.vector.tensor_tensor(faded[:], old_sb[b][:].indirect(offsets[:]), lost[:], ALU.mult)
+            finish(b - 1, 1, "codes%d" % b)
+            scatter(b, faded, minus_a)
+        finish(BLOCKS - 1, LAST_PIECES)

@@ -1,6 +1,7 @@
 from contextlib import ExitStack
 
 import concourse.mybir as mybir
+from concourse.masks import make_identity
 
 K, T, J, N = 1024, 1024, 512, 512
 FLOPS = 2 * 2 * K * N * J
@@ -21,6 +22,7 @@ PACK = 4
 PASSES = K // (P * PACK)
 BLOCKS = N // P
 LAST_PIECES = 2
+BANK = 512
 
 
 def tile_moe_expert_page_fades_where_written_kernel(tc, xt_words, xt_scales, wa, wg_words, wg_scales, old, offs, out):
@@ -39,7 +41,11 @@ def tile_moe_expert_page_fades_where_written_kernel(tc, xt_words, xt_scales, wa,
         x_plane = sbuf([P, PASSES * T], U8, "x_plane")
         g_plane = sbuf([P, PASSES * N], U8, "g_plane")
         pages = [sbuf([P, T], F32, "page%d" % i) for i in range(2)]
+        first_page = sbuf([P, T], F32, "first_page")
+        ident = sbuf([P, P], F32, "ident")
         nc.gpsimd.memset(x_plane[:].bitcast(I32), 0)
+        nc.gpsimd.memset(first_page[:], 0.0)
+        make_identity(nc, ident[:])
         nc.vector.memset(g_plane[:].bitcast(I32), 0)
         for page in pages:
             nc.vector.memset(page[:], 0.0)
@@ -123,18 +129,36 @@ def tile_moe_expert_page_fades_where_written_kernel(tc, xt_words, xt_scales, wa,
             nc.scalar.activation(lost[:], acc[:], ACT.Sigmoid, scale=-1.0)
             return lost
 
-        def expert(b, codes, plane):
+        def expert(b, codes, plane, sign):
             acc = product(
                 (b + 1) % 2,
                 [codes[:, a * P : (a + 1) * P].bitcast(FP8X4) for a in range(PASSES)],
                 [plane[:, a * P : (a + 1) * P] for a in range(PASSES)],
             )
-            minus_a = sbuf([P, J], F32, "minus_a%d" % b)
-            nc.scalar.activation(minus_a[:], acc[:], ACT.Copy, scale=-1.0)
-            return minus_a
+            answer = sbuf([P, J], F32, "answer%d" % b)
+            nc.scalar.activation(answer[:], acc[:], ACT.Copy, scale=sign)
+            return answer
 
-        def scatter(b, faded, minus_a):
-            nc.vector.tensor_tensor(pages[b % 2][:].indirect(offsets[:]), faded[:], minus_a[:], ALU.add)
+        def scatter(page, faded, answer):
+            nc.vector.tensor_tensor(page[:].indirect(offsets[:]), faded[:], answer[:], ALU.add)
+
+        def finish_first():
+            halves = [slice(first, first + BANK) for first in range(0, T, BANK)]
+            turned = sums.tile([P, T], F32, name="turned", tag="bank1")
+            turned_sb = sbuf([P, T], F32, "turned_sb")
+            for cols in halves:
+                for c in range(cols.start, cols.stop, P):
+                    src = slice(c, c + P)
+                    nc.tensor.matmul(turned[:, src], old_sb[0][:, src], ident[:], start=True, stop=False, is_transpose=True)
+                    nc.tensor.matmul(turned[:, src], first_page[:, src], ident[:], start=False, stop=True, is_transpose=True)
+                nc.scalar.copy(turned_sb[:, cols], turned[:, cols])
+            back = sums.tile([P, T], F32, name="back")
+            for cols in halves:
+                for c in range(cols.start, cols.stop, P):
+                    nc.tensor.transpose(back[:, c : c + P], turned_sb[:, c : c + P], ident[:])
+                result = sbuf([P, BANK], F32, "result0_%d" % cols.start)
+                nc.scalar.copy(result[:], back[:, cols])
+                nc.scalar.dma_start(out[0:P, cols], result[:])
 
         def finish(b, pieces, place=None):
             width = T // pieces
@@ -144,27 +168,46 @@ def tile_moe_expert_page_fades_where_written_kernel(tc, xt_words, xt_scales, wa,
                 nc.vector.tensor_tensor(result[:], old_sb[b][:, cols], pages[b % 2][:, cols], ALU.subtract)
                 nc.sync.dma_start(out[b * P : (b + 1) * P, cols], result[:])
 
-        rounded = cast(0, [raw[:] for raw in first_raw], "rounded0")
-        codes, plane = quantise(0, rounded)
-        lost = gate(0, "first_raw1")
-        minus_a = expert(0, codes, plane)
+        def fade(b, lost):
+            faded = sbuf([P, J], F32, "faded%d" % b)
+            nc.vector.tensor_tensor(faded[:], old_sb[b][:].indirect(offsets[:]), lost[:], ALU.mult)
+            return faded
+
+        def rest(b):
+            return [raw[:, :, (b - 1) * P : b * P] for raw in rest_raw]
+
+        packed0 = quantise(0, cast(0, [raw[:] for raw in first_raw], "rounded0"))
+        lost0 = gate(0, "first_raw1")
+        answer0 = expert(0, *packed0, 1.0)
         picked = sbuf([P, J], F32, "picked", "rounded0")
         nc.vector.tensor_copy(picked[:], old_sb[0][:].indirect(offsets[:]))
-        faded = sbuf([P, J], F32, "faded0")
-        nc.vector.tensor_tensor(faded[:], lost[:], picked[:], ALU.mult)
-        scatter(0, faded, minus_a)
+        faded0 = sbuf([P, J], F32, "faded0")
+        nc.vector.scalar_tensor_tensor(faded0[:], lost0[:], -1.0, picked[:], ALU.mult, ALU.mult)
+        scatter(first_page, faded0, answer0)
 
         rest_raw = [load_wa(0, P, N - P, "rest_raw0", "first_raw0"), load_wa(1, P, N - P, "rest_raw1", "x_plane")]
         for b, place in enumerate(["x_words", "rounded0", "first_raw1"], start=1):
             old_sb[b] = load_old(b, place)
 
-        for b in range(1, BLOCKS):
-            rounded = cast(b, [raw[:, :, (b - 1) * P : b * P] for raw in rest_raw], "w_plane%d" % (b - 1))
-            lost = gate(b)
-            codes, plane = quantise(b, rounded)
-            minus_a = expert(b, codes, plane)
-            faded = sbuf([P, J], F32, "faded%d" % b)
-            nc.vector.tensor_tensor(faded[:], old_sb[b][:].indirect(offsets[:]), lost[:], ALU.mult)
-            finish(b - 1, 1, "codes%d" % b)
-            scatter(b, faded, minus_a)
-        finish(BLOCKS - 1, LAST_PIECES)
+        rounded1 = cast(1, rest(1), "w_plane0")
+        lost1 = gate(1)
+        packed1 = quantise(1, rounded1)
+        rounded2 = cast(2, rest(2), "codes0")
+        answer1 = expert(1, *packed1, -1.0)
+        faded1 = fade(1, lost1)
+        packed2 = quantise(2, rounded2)
+        scatter(pages[1], faded1, answer1)
+
+        packed3 = quantise(3, cast(3, rest(3), "w_plane1"))
+        lost2 = gate(2)
+        answer2 = expert(2, *packed2, -1.0)
+        lost3 = gate(3)
+        answer3 = expert(3, *packed3, -1.0)
+        faded2 = fade(2, lost2)
+        finish(1, 1, "codes3")
+        scatter(pages[0], faded2, answer2)
+        finish_first()
+        faded3 = fade(3, lost3)
+        finish(2, 1, "lost3")
+        scatter(pages[1], faded3, answer3)
+        finish(3, LAST_PIECES)

from contextlib import ExitStack

import concourse.mybir as mybir
from concourse.masks import make_identity

K, T, J, N = 1024, 1024, 512, 512
FLOPS = 2 * 2 * K * N * J

F32 = mybir.dt.float32
BF16 = mybir.dt.bfloat16
I32 = mybir.dt.int32
U32 = mybir.dt.uint32
U16 = mybir.dt.uint16
U8 = mybir.dt.uint8
FP8X4 = mybir.dt.float8_e4m3fn_x4
FP4X4 = mybir.dt.float4_e2m1fn_x4
ACT = mybir.ActivationFunctionType
ALU = mybir.AluOpType

P = 128
PACK = 4
PASSES = K // (P * PACK)
BLOCKS = N // P
LAST_PIECES = 2
BANK = 512


def tile_moe_expert_page_fades_where_written_kernel(tc, xt_words, xt_scales, wa, wg_words, wg_scales, old, offs, out):
    nc = tc.nc
    with ExitStack() as ctx:
        lists = ctx.enter_context(tc.tile_pool(name="lists", bufs=1))
        keep = ctx.enter_context(tc.tile_pool(name="keep", bufs=1))
        sums = ctx.enter_context(tc.psum_pool(name="sums", bufs=1))

        def sbuf(shape, dtype, name, place=None):
            return keep.tile(shape, dtype, name=name, tag=place or name, align_bytes=64)

        offsets = lists.tile([P, J // 16], U16, name="offsets")
        nc.sync.dma_start(offsets[:], offs)

        x_plane = sbuf([P, PASSES * T], U8, "x_plane")
        g_plane = sbuf([P, PASSES * N], U8, "g_plane")
        pages = [sbuf([P, T], F32, "page%d" % i) for i in range(2)]
        first_page = sbuf([P, T], F32, "first_page")
        ident = sbuf([P, P], F32, "ident")
        nc.gpsimd.memset(x_plane[:].bitcast(I32), 0)
        nc.gpsimd.memset(first_page[:], 0.0)
        make_identity(nc, ident[:])
        nc.vector.memset(g_plane[:].bitcast(I32), 0)
        for page in pages:
            nc.vector.memset(page[:], 0.0)
        warm = sbuf([P, 1], F32, "warm")
        nc.scalar.activation(warm[:], pages[0][:, 0:1], ACT.Sigmoid)

        def load_scale_rows(plane, scales):
            rows = scales.bitcast(I32)
            for q in range(4):
                nc.sync.dma_start(
                    plane[32 * q : 32 * q + 4, :].bitcast(I32).rearrange("r (a n) -> r a n", a=PASSES),
                    rows[:, 4 * q : 4 * q + 4, :].rearrange("a r n -> r a n"),
                )

        def load_wa(a, first, count, name, place=None):
            raw = sbuf([P, PACK, count], F32, name, place)
            rows = wa[a * P * PACK : (a + 1) * P * PACK, first : first + count]
            nc.sync.dma_start(raw[:], rows.rearrange("(p j) n -> p j n", j=PACK))
            return raw

        def load_old(b, place=None):
            rows = sbuf([P, T], F32, "old%d" % b, place)
            nc.sync.dma_start(rows[:], old[b * P : (b + 1) * P, :])
            return rows

        g_words = sbuf([P, PASSES, 2 * N], U8, "g_words")
        nc.sync.dma_start(g_words[:].bitcast(I32), wg_words.bitcast(I32).rearrange("a p n -> p a n"))
        load_scale_rows(x_plane, xt_scales)
        x_words = sbuf([P, PASSES, T], U32, "x_words")
        nc.sync.dma_start(x_words[:].bitcast(I32), xt_words.rearrange("a p n t -> p a (n t)").bitcast(I32))
        first_raw = [load_wa(0, 0, P, "first_raw0")]
        load_scale_rows(g_plane, wg_scales)
        first_raw.append(load_wa(1, 0, P, "first_raw1"))
        old_sb = {0: load_old(0)}

        xg_plane = [sbuf([P, J], U8, "xg_plane%d" % a) for a in range(PASSES)]
        xg_words = [sbuf([P, J], U32, "xg_words%d" % a) for a in range(PASSES)]
        for a in range(PASSES):
            nc.vector.tensor_copy(xg_plane[a][:], x_plane[:, a * T : (a + 1) * T].indirect(offsets[:]))
        for a in range(PASSES):
            nc.vector.tensor_copy(xg_words[a][:], x_words[:, a, :].indirect(offsets[:]))

        def cast(b, raw, place):
            rounded = sbuf([P, PASSES, P * PACK], BF16, "rounded%d" % b, place)
            for a in range(PASSES):
                nc.scalar.copy(
                    rounded[:, a, :].rearrange("p (c i t) -> p c t i", i=4, t=PACK),
                    raw[a].rearrange("p t (c i) -> p c t i", i=4),
                )
            return rounded

        def quantise(b, rounded):
            codes = sbuf([P, PASSES * P], U32, "codes%d" % b)
            plane = sbuf([P, PASSES * P], U8, "w_plane%d" % b)
            nc.vector.quantize_mx(
                out=codes[:].bitcast(FP8X4), scales=plane[:], in_=rounded[:].rearrange("p a c -> p (a c)")
            )
            return codes, plane

        def product(bank, weights, scales):
            acc = sums.tile([P, J], F32, name="acc", tag="bank%d" % bank)
            for a in range(PASSES):
                nc.tensor.matmul_mx(
                    out=acc[:],
                    lhsT=weights[a],
                    lhsT_scale=scales[a],
                    rhs=xg_words[a][:].bitcast(FP8X4),
                    rhs_scale=xg_plane[a][:],
                    start=(a == 0),
                    stop=(a == PASSES - 1),
                )
            return acc

        def gate(b, place=None):
            acc = product(
                b % 2,
                [g_words[:, a, 2 * b * P : 2 * (b + 1) * P].bitcast(FP4X4) for a in range(PASSES)],
                [g_plane[:, a * N + b * P : a * N + (b + 1) * P] for a in range(PASSES)],
            )
            lost = sbuf([P, J], F32, "lost%d" % b, place)
            nc.scalar.activation(lost[:], acc[:], ACT.Sigmoid, scale=-1.0)
            return lost

        def expert(b, codes, plane, sign):
            acc = product(
                (b + 1) % 2,
                [codes[:, a * P : (a + 1) * P].bitcast(FP8X4) for a in range(PASSES)],
                [plane[:, a * P : (a + 1) * P] for a in range(PASSES)],
            )
            answer = sbuf([P, J], F32, "answer%d" % b)
            nc.scalar.activation(answer[:], acc[:], ACT.Copy, scale=sign)
            return answer

        def scatter(page, faded, answer):
            nc.vector.tensor_tensor(page[:].indirect(offsets[:]), faded[:], answer[:], ALU.add)

        def finish_first():
            halves = [slice(first, first + BANK) for first in range(0, T, BANK)]
            turned = sums.tile([P, T], F32, name="turned", tag="bank1")
            turned_sb = sbuf([P, T], F32, "turned_sb")
            for cols in halves:
                for c in range(cols.start, cols.stop, P):
                    src = slice(c, c + P)
                    nc.tensor.matmul(turned[:, src], old_sb[0][:, src], ident[:], start=True, stop=False, is_transpose=True)
                    nc.tensor.matmul(turned[:, src], first_page[:, src], ident[:], start=False, stop=True, is_transpose=True)
                nc.scalar.copy(turned_sb[:, cols], turned[:, cols])
            back = sums.tile([P, T], F32, name="back")
            for cols in halves:
                for c in range(cols.start, cols.stop, P):
                    nc.tensor.transpose(back[:, c : c + P], turned_sb[:, c : c + P], ident[:])
                result = sbuf([P, BANK], F32, "result0_%d" % cols.start)
                nc.scalar.copy(result[:], back[:, cols])
                nc.scalar.dma_start(out[0:P, cols], result[:])

        def finish(b, pieces, place=None):
            width = T // pieces
            for first in range(0, T, width):
                cols = slice(first, first + width)
                result = sbuf([P, width], F32, "result%d_%d" % (b, first), place)
                nc.vector.tensor_tensor(result[:], old_sb[b][:, cols], pages[b % 2][:, cols], ALU.subtract)
                nc.sync.dma_start(out[b * P : (b + 1) * P, cols], result[:])

        def fade(b, lost):
            faded = sbuf([P, J], F32, "faded%d" % b)
            nc.vector.tensor_tensor(faded[:], old_sb[b][:].indirect(offsets[:]), lost[:], ALU.mult)
            return faded

        def rest(b):
            return [raw[:, :, (b - 1) * P : b * P] for raw in rest_raw]

        packed0 = quantise(0, cast(0, [raw[:] for raw in first_raw], "rounded0"))
        lost0 = gate(0, "first_raw1")
        answer0 = expert(0, *packed0, 1.0)
        picked = sbuf([P, J], F32, "picked", "rounded0")
        nc.vector.tensor_copy(picked[:], old_sb[0][:].indirect(offsets[:]))
        faded0 = sbuf([P, J], F32, "faded0")
        nc.vector.scalar_tensor_tensor(faded0[:], lost0[:], -1.0, picked[:], ALU.mult, ALU.mult)
        scatter(first_page, faded0, answer0)

        rest_raw = [load_wa(0, P, N - P, "rest_raw0", "first_raw0"), load_wa(1, P, N - P, "rest_raw1", "x_plane")]
        for b, place in enumerate(["x_words", "rounded0", "first_raw1"], start=1):
            old_sb[b] = load_old(b, place)

        rounded1 = cast(1, rest(1), "w_plane0")
        lost1 = gate(1)
        packed1 = quantise(1, rounded1)
        rounded2 = cast(2, rest(2), "codes0")
        answer1 = expert(1, *packed1, -1.0)
        faded1 = fade(1, lost1)
        packed2 = quantise(2, rounded2)
        scatter(pages[1], faded1, answer1)

        packed3 = quantise(3, cast(3, rest(3), "w_plane1"))
        lost2 = gate(2)
        answer2 = expert(2, *packed2, -1.0)
        lost3 = gate(3)
        answer3 = expert(3, *packed3, -1.0)
        faded2 = fade(2, lost2)
        finish(1, 1, "codes3")
        scatter(pages[0], faded2, answer2)
        finish_first()
        faded3 = fade(3, lost3)
        finish(2, 1, "lost3")
        scatter(pages[1], faded3, answer3)
        finish(3, LAST_PIECES)
